import numpy as np
import ml_dtypes


def mxq(x, axis, fmt="e4m3"):
    dtype, down = {"e4m3": (ml_dtypes.float8_e4m3fn, 7), "e5m2": (ml_dtypes.float8_e5m2, 14)}[fmt]
    v = np.moveaxis(np.asarray(x, np.float32).astype(ml_dtypes.bfloat16).astype(np.float64), axis, -1)
    blocks = v.reshape(v.shape[:-1] + (-1, 32))
    amax = np.abs(blocks).max(-1, keepdims=True)
    byte = np.maximum(np.where(amax > 0, np.frexp(amax)[1] - 1 + 127, 0) - down, 1)
    scale = np.exp2(byte - 127.0)
    codes = (blocks / scale).astype(np.float32).astype(dtype).astype(np.float64)
    return np.moveaxis((codes * scale).reshape(v.shape), -1, axis)


WIDE = False


def mx_kscale(k):
    if not WIDE:
        return np.ones(k)
    levels = np.array([10, -10, 5, -5, 0])
    if k % 512:
        return np.exp2(np.random.permutation(np.resize(levels, k // 32))).repeat(32)
    a = np.empty((k // 512, 16))
    for p in range(k // 512):
        a[p, :8] = np.random.permutation(np.resize(levels, 8))
        for g in range(8):
            far = levels[np.abs(levels - a[p, g]) >= 10]
            a[p, g + 8] = far[np.random.randint(len(far))]
    return np.exp2(a.ravel()).repeat(32)


def f64(x):
    return np.asarray(x).astype(np.float64)


def striped(idx):
    return np.tile(idx.reshape(-1, 16).T, (8, 1)).astype(np.uint16)


def unstriped(offs):
    return offs[:16].T.reshape(-1).astype(np.int64)


def pack_weight(w):
    k, n = w.shape
    w = f64(np.asarray(w, np.float32).astype(ml_dtypes.bfloat16)).reshape(k // 32, 32, n)
    amax = np.abs(w).max(1)
    byte = np.clip(np.where(amax > 0, np.frexp(amax)[1] - 1 + 127 - 7, 1), 1, 254)
    scaled = (w * np.exp2(127.0 - byte)[:, None, :]).reshape(k, n).astype(np.float32)
    words = np.ascontiguousarray(scaled.reshape(k // 512, 128, 4, n).transpose(0, 1, 3, 2)).astype(ml_dtypes.float8_e4m3fn).view(np.uint8)
    return words, np.ascontiguousarray(byte.astype(np.uint8).reshape(k // 512, 16, n))


def unpack_weight(words, scales):
    g, p, n, _ = words.shape
    vals = np.ascontiguousarray(words).view(ml_dtypes.float8_e4m3fn).astype(np.float64) * np.repeat(np.exp2(scales.astype(np.float64) - 127.0), 8, axis=1)[..., None]
    return vals.transpose(0, 1, 3, 2).reshape(g * 512, n)


def silu(v):
    return v / (1.0 + np.exp(-np.maximum(v, -700.0)))


K, T, D, S, V, N = 1536, 1024, 8, 512, 64, 128


def setup_inputs():
    n = np.random.standard_normal
    s = mx_kscale(K)[:, None]
    words, scales = pack_weight(n((K, N)) / np.sqrt(K) / s)
    return {
        "xT": (n((K, T)) * s).astype(np.float32),
        "w_words": words,
        "w_scales": scales,
        "b": (0.3 * n((N, 1))).astype(np.float32),
        "offs": striped(np.random.permutation(T)[:S]),
    }


def reference(xT, w_words, w_scales, b, offs):
    w = unpack_weight(w_words, w_scales)
    idx = unstriped(offs)
    xq = mxq(f64(xT)[:, idx], 0, "e4m3")
    y = w.T @ xq
    y = silu(y + f64(b))
    return y.reshape(N, V, D).max(axis=2)

@@ -1,0 +1,136 @@
+from contextlib import ExitStack
+
+import concourse.mybir as mybir
+
+K, T, D, S, V, N = 1536, 1024, 8, 512, 64, 128
+FLOPS = 2 * K * N * S
+
+F32 = mybir.dt.float32
+BF16 = mybir.dt.bfloat16
+I32 = mybir.dt.int32
+U32 = mybir.dt.uint32
+U16 = mybir.dt.uint16
+U8 = mybir.dt.uint8
+FP8X4 = mybir.dt.float8_e4m3fn_x4
+SILU = mybir.ActivationFunctionType.Silu
+
+P = 128
+PACK = 4
+K_PASS = P * PACK
+PASSES = K // K_PASS
+PAIRS = 2 * PASSES
+SLICES = ((0, 256), (256, 384), (384, 512))
+
+
+def load_chunks(pair):
+    if pair == PAIRS - 1:
+        return ((0, 512), (512, 768), (768, 1024))
+    return ((0, 512), (512, 1024))
+
+
+def scalar_end(pair):
+    return 768 if pair == PAIRS - 1 else 896
+
+
+def tile_picked_pool_lin_silu_sub_e_kernel(tc, xT, w_words, w_scales, b, offs, out):
+    nc = tc.nc
+    with ExitStack() as ctx:
+        keep = ctx.enter_context(tc.tile_pool(name="keep", bufs=1))
+        psum = ctx.enter_context(tc.psum_pool(name="psum", bufs=1))
+
+        offsets = keep.tile([P, S // 16], U16, name="offsets")
+        w_codes = keep.tile([P, PASSES, N], U32, name="w_codes", align_bytes=64)
+        w_plane = keep.tile([P, PASSES, N], U8, name="w_plane", align_bytes=64)
+        bias = keep.tile([P, 1], F32, name="bias")
+        warm = keep.tile([P, 2], F32, name="warm")
+        pooled = keep.tile([P, V], F32, name="pooled")
+        raw = [keep.tile([P, 2, T], F32, name=f"raw{i}") for i in range(PAIRS)]
+        words = [keep.tile([P, T, 2], BF16, name=f"words{i}", align_bytes=64) for i in range(PAIRS)]
+        picked = [keep.tile([P, S, PACK], BF16, name=f"picked{a}", align_bytes=64) for a in range(PASSES)]
+        x_codes = [keep.tile([P, S], U32, name=f"x_codes{a}", align_bytes=64) for a in range(PASSES)]
+        x_plane = [keep.tile([P, S], U8, name=f"x_plane{a}", align_bytes=64) for a in range(PASSES)]
+        acc = [psum.tile([P, hi - lo], F32, name=f"acc{lo}") for lo, hi in SLICES]
+        act = [keep.tile([P, hi - lo], F32, name=f"act{lo}") for lo, hi in SLICES]
+
+        nc.vector.memset(warm[:, 0:1], 0.0)
+        nc.vector.memset(w_plane[:].rearrange("p a n -> p (a n)").bitcast(I32), 0)
+        nc.scalar.activation(warm[:, 1:2], warm[:, 0:1], SILU)
+
+        x_rows = xT.rearrange("(a p u e) t -> a u p e t", a=PASSES, p=P, u=2)
+
+        def load(i):
+            for lo, hi in load_chunks(i):
+                nc.sync.dma_start(out=raw[i][:, :, lo:hi], in_=x_rows[i // 2, i % 2][:, :, lo:hi])
+
+        load(0)
+        nc.sync.dma_start(offsets[:], offs)
+        load(1)
+        nc.sync.dma_start(
+            out=w_codes[:].bitcast(I32),
+            in_=w_words.rearrange("a p n r -> p a (n r)").bitcast(I32),
+        )
+        scale_rows = w_scales.bitcast(I32).rearrange("a (q r) n -> r q a n", r=4)
+        for r in range(4):
+            nc.sync.dma_start(out=w_plane[r:P:32].bitcast(I32), in_=scale_rows[r])
+        nc.sync.dma_start(out=bias[:], in_=b)
+        for i in range(2, PAIRS):
+            load(i)
+
+        def round_pair(i):
+            cut = scalar_end(i)
+            for lo, hi in load_chunks(i):
+                hi = min(hi, cut)
+                if lo < hi:
+                    nc.scalar.copy(words[i][:, lo:hi, :], raw[i][:, :, lo:hi].rearrange("p e t -> p t e"))
+            nc.vector.tensor_copy(words[i][:, cut:, :], raw[i][:, :, cut:].rearrange("p e t -> p t e"))
+
+        def gather(i, lo, hi):
+            window = words[i][:].rearrange("p t e -> p (t e)").bitcast(U32)
+            dst = picked[i // 2][:].rearrange("p s j -> p (s j)").bitcast(U32).rearrange("p (s u) -> p s u", u=2)
+            nc.vector.tensor_copy(dst[:, lo:hi, i % 2], window.indirect(offsets[:, lo // 16 : hi // 16]))
+
+        def quantize(a, lo, hi):
+            nc.vector.quantize_mx(
+                out=x_codes[a][:, lo:hi].bitcast(FP8X4),
+                scales=x_plane[a][:, lo:hi],
+                in_=picked[a][:, lo:hi, :].rearrange("p s j -> p (s j)"),
+            )
+
+        def multiply(a, s):
+            lo, hi = SLICES[s]
+            nc.tensor.matmul_mx(
+                out=acc[s][:],
+                lhsT=w_codes[:, a, :].bitcast(FP8X4),
+                lhsT_scale=w_plane[:, a, :],
+                rhs=x_codes[a][:, lo:hi].bitcast(FP8X4),
+                rhs_scale=x_plane[a][:, lo:hi],
+                start=(a == 0),
+                stop=(a == PASSES - 1),
+            )
+
+        for i in range(PAIRS - 1):
+            round_pair(i)
+            if i > 0 and i % 2 == 0:
+                a = i // 2 - 1
+                quantize(a, 0, S)
+                for s in range(len(SLICES)):
+                    multiply(a, s)
+            gather(i, 0, S)
+
+        last = PASSES - 1
+        round_pair(PAIRS - 1)
+        gather(PAIRS - 1, *SLICES[0])
+        for s in range(len(SLICES)):
+            if s + 1 < len(SLICES):
+                gather(PAIRS - 1, *SLICES[s + 1])
+            quantize(last, *SLICES[s])
+            multiply(last, s)
+            nc.scalar.activation(act[s][:], acc[s][:], SILU, bias=bias[:])
+        for s, (lo, hi) in enumerate(SLICES):
+            nc.vector.tensor_reduce(
+                out=pooled[:, lo // D : hi // D],
+                in_=act[s][:].rearrange("p (v d) -> p v d", d=D),
+                axis=mybir.AxisListType.X,
+                op=mybir.AluOpType.max,
+            )
+        nc.sync.dma_start(out=out, in_=pooled[:])

@@ -19,17 +19,14 @@ PACK = 4
 K_PASS = P * PACK
 PASSES = K // K_PASS
 PAIRS = 2 * PASSES
-SLICES = ((0, 256), (256, 384), (384, 512))
+SLICES = ((0, 128), (128, 256), (256, 384), (384, 512))
+VECTOR_SHARE = (512, 320, 192, 256, 0, 384)
 
 
 def load_chunks(pair):
-    if pair == PAIRS - 1:
-        return ((0, 512), (512, 768), (768, 1024))
-    return ((0, 512), (512, 1024))
-
-
-def scalar_end(pair):
-    return 768 if pair == PAIRS - 1 else 896
+    if pair < 3:
+        return ((0, T),)
+    return ((0, T // 2), (T // 2, T))
 
 
 def tile_picked_pool_lin_silu_sub_e_kernel(tc, xT, w_words, w_scales, b, offs, out):
@@ -46,6 +43,7 @@ def tile_picked_pool_lin_silu_sub_e_kernel(tc, xT, w_words, w_scales, b, offs, o
         pooled = keep.tile([P, V], F32, name="pooled")
         raw = [keep.tile([P, 2, T], F32, name=f"raw{i}") for i in range(PAIRS)]
         words = [keep.tile([P, T, 2], BF16, name=f"words{i}", align_bytes=64) for i in range(PAIRS)]
+        halves = [keep.tile([P, 2, S], U32, name=f"halves{a}", align_bytes=64) for a in range(PASSES)]
         picked = [keep.tile([P, S, PACK], BF16, name=f"picked{a}", align_bytes=64) for a in range(PASSES)]
         x_codes = [keep.tile([P, S], U32, name=f"x_codes{a}", align_bytes=64) for a in range(PASSES)]
         x_plane = [keep.tile([P, S], U8, name=f"x_plane{a}", align_bytes=64) for a in range(PASSES)]
@@ -64,7 +62,8 @@ def tile_picked_pool_lin_silu_sub_e_kernel(tc, xT, w_words, w_scales, b, offs, o
 
         load(0)
         nc.sync.dma_start(offsets[:], offs)
-        load(1)
+        for i in range(1, PAIRS):
+            load(i)
         nc.sync.dma_start(
             out=w_codes[:].bitcast(I32),
             in_=w_words.rearrange("a p n r -> p a (n r)").bitcast(I32),
@@ -73,21 +72,24 @@ def tile_picked_pool_lin_silu_sub_e_kernel(tc, xT, w_words, w_scales, b, offs, o
         for r in range(4):
             nc.sync.dma_start(out=w_plane[r:P:32].bitcast(I32), in_=scale_rows[r])
         nc.sync.dma_start(out=bias[:], in_=b)
-        for i in range(2, PAIRS):
-            load(i)
 
         def round_pair(i):
-            cut = scalar_end(i)
+            cut = T - VECTOR_SHARE[i]
             for lo, hi in load_chunks(i):
                 hi = min(hi, cut)
                 if lo < hi:
                     nc.scalar.copy(words[i][:, lo:hi, :], raw[i][:, :, lo:hi].rearrange("p e t -> p t e"))
-            nc.vector.tensor_copy(words[i][:, cut:, :], raw[i][:, :, cut:].rearrange("p e t -> p t e"))
+            if cut < T:
+                nc.vector.tensor_copy(words[i][:, cut:, :], raw[i][:, :, cut:].rearrange("p e t -> p t e"))
 
         def gather(i, lo, hi):
             window = words[i][:].rearrange("p t e -> p (t e)").bitcast(U32)
-            dst = picked[i // 2][:].rearrange("p s j -> p (s j)").bitcast(U32).rearrange("p (s u) -> p s u", u=2)
-            nc.vector.tensor_copy(dst[:, lo:hi, i % 2], window.indirect(offsets[:, lo // 16 : hi // 16]))
+            nc.vector.tensor_copy(halves[i // 2][:, i % 2, lo:hi], window.indirect(offsets[:, lo // 16 : hi // 16]))
+
+        def interleave(copy, a, lo, hi):
+            src = halves[a][:].bitcast(BF16).rearrange("p u (s e) -> p s u e", e=2)
+            dst = picked[a][:].rearrange("p s (u e) -> p s u e", e=2)
+            copy(dst[:, lo:hi], src[:, lo:hi])
 
         def quantize(a, lo, hi):
             nc.vector.quantize_mx(
@@ -109,20 +111,23 @@ def tile_picked_pool_lin_silu_sub_e_kernel(tc, xT, w_words, w_scales, b, offs, o
             )
 
         for i in range(PAIRS - 1):
+            finished = i // 2 - 1 if i > 0 and i % 2 == 0 else None
+            if finished is not None:
+                interleave(nc.vector.tensor_copy, finished, 0, S)
             round_pair(i)
-            if i > 0 and i % 2 == 0:
-                a = i // 2 - 1
-                quantize(a, 0, S)
-                for s in range(len(SLICES)):
-                    multiply(a, s)
+            if finished is not None:
+                quantize(finished, 0, S)
             gather(i, 0, S)
 
         last = PASSES - 1
         round_pair(PAIRS - 1)
-        gather(PAIRS - 1, *SLICES[0])
         for s in range(len(SLICES)):
-            if s + 1 < len(SLICES):
-                gather(PAIRS - 1, *SLICES[s + 1])
+            for a in range(last):
+                multiply(a, s)
+        for lo, hi in SLICES:
+            gather(PAIRS - 1, lo, hi)
+            interleave(nc.scalar.copy, last, lo, hi)
+        for s in range(len(SLICES)):
             quantize(last, *SLICES[s])
             multiply(last, s)
             nc.scalar.activation(act[s][:], acc[s][:], SILU, bias=bias[:])

@@ -20,11 +20,12 @@ K_PASS = P * PACK
 PASSES = K // K_PASS
 PAIRS = 2 * PASSES
 SLICES = ((0, 128), (128, 256), (256, 384), (384, 512))
-VECTOR_SHARE = (512, 320, 192, 256, 0, 384)
+VECTOR_SHARE = (704, 672, 320, 448, 0, 320)
+HALVES = ((0, S // 2), (S // 2, S))
 
 
 def load_chunks(pair):
-    if pair < 3:
+    if pair < 4:
         return ((0, T),)
     return ((0, T // 2), (T // 2, T))
 
@@ -87,8 +88,8 @@ def tile_picked_pool_lin_silu_sub_e_kernel(tc, xT, w_words, w_scales, b, offs, o
             nc.vector.tensor_copy(halves[i // 2][:, i % 2, lo:hi], window.indirect(offsets[:, lo // 16 : hi // 16]))
 
         def interleave(copy, a, lo, hi):
-            src = halves[a][:].bitcast(BF16).rearrange("p u (s e) -> p s u e", e=2)
-            dst = picked[a][:].rearrange("p s (u e) -> p s u e", e=2)
+            src = halves[a][:].bitcast(F32).rearrange("p u s -> p s u")
+            dst = picked[a][:].bitcast(F32)
             copy(dst[:, lo:hi], src[:, lo:hi])
 
         def quantize(a, lo, hi):
@@ -110,16 +111,20 @@ def tile_picked_pool_lin_silu_sub_e_kernel(tc, xT, w_words, w_scales, b, offs, o
                 stop=(a == PASSES - 1),
             )
 
-        for i in range(PAIRS - 1):
-            finished = i // 2 - 1 if i > 0 and i % 2 == 0 else None
-            if finished is not None:
-                interleave(nc.vector.tensor_copy, finished, 0, S)
-            round_pair(i)
-            if finished is not None:
-                quantize(finished, 0, S)
-            gather(i, 0, S)
-
         last = PASSES - 1
+        round_pair(0)
+        gather(0, 0, S)
+        for a in range(last):
+            round_pair(2 * a + 1)
+            for lo, hi in HALVES:
+                gather(2 * a + 1, lo, hi)
+            round_pair(2 * a + 2)
+            for lo, hi in HALVES:
+                interleave(nc.vector.tensor_copy, a, lo, hi)
+            for lo, hi in HALVES:
+                quantize(a, lo, hi)
+            gather(2 * a + 2, 0, S)
+
         round_pair(PAIRS - 1)
         for s in range(len(SLICES)):
             for a in range(last):

@@ -20,14 +20,18 @@ K_PASS = P * PACK
 PASSES = K // K_PASS
 PAIRS = 2 * PASSES
 SLICES = ((0, 128), (128, 256), (256, 384), (384, 512))
-VECTOR_SHARE = (704, 672, 320, 448, 0, 320)
-HALVES = ((0, S // 2), (S // 2, S))
+VECTOR_SHARE = (704, 672, 64, 0, 0, 96)
+
+
+GPSIMD_SHARE = {(3, 0): 384, (4, 0): 128, (4, 512): 96, (5, 512): 160}
 
 
 def load_chunks(pair):
     if pair < 4:
         return ((0, T),)
-    return ((0, T // 2), (T // 2, T))
+    if pair == 4:
+        return ((0, T // 2), (T // 2, T))
+    return ((0, T // 2), (T // 2, 3 * T // 4), (3 * T // 4, T))
 
 
 def tile_picked_pool_lin_silu_sub_e_kernel(tc, xT, w_words, w_scales, b, offs, out):
@@ -74,14 +78,25 @@ def tile_picked_pool_lin_silu_sub_e_kernel(tc, xT, w_words, w_scales, b, offs, o
             nc.sync.dma_start(out=w_plane[r:P:32].bitcast(I32), in_=scale_rows[r])
         nc.sync.dma_start(out=bias[:], in_=b)
 
-        def round_pair(i):
+        def round_scalar(i):
             cut = T - VECTOR_SHARE[i]
             for lo, hi in load_chunks(i):
                 hi = min(hi, cut)
-                if lo < hi:
-                    nc.scalar.copy(words[i][:, lo:hi, :], raw[i][:, :, lo:hi].rearrange("p e t -> p t e"))
-            if cut < T:
-                nc.vector.tensor_copy(words[i][:, cut:, :], raw[i][:, :, cut:].rearrange("p e t -> p t e"))
+                mid = hi - GPSIMD_SHARE.get((i, lo), 0)
+                nc.scalar.copy(words[i][:, lo:mid, :], raw[i][:, :, lo:mid].rearrange("p e t -> p t e"))
+                if mid < hi:
+                    nc.gpsimd.tensor_scalar(
+                        words[i][:, mid:hi, :],
+                        raw[i][:, :, mid:hi].rearrange("p e t -> p t e"),
+                        1.0,
+                        0.0,
+                        mybir.AluOpType.mult,
+                        mybir.AluOpType.add,
+                    )
+
+        def round_vector(i):
+            cut = T - VECTOR_SHARE[i]
+            nc.vector.tensor_copy(words[i][:, cut:, :], raw[i][:, :, cut:].rearrange("p e t -> p t e"))
 
         def gather(i, lo, hi):
             window = words[i][:].rearrange("p t e -> p (t e)").bitcast(U32)
@@ -112,20 +127,31 @@ def tile_picked_pool_lin_silu_sub_e_kernel(tc, xT, w_words, w_scales, b, offs, o
             )
 
         last = PASSES - 1
-        round_pair(0)
+        round_scalar(0)
+        round_vector(0)
+        round_scalar(1)
+        round_scalar(2)
+        round_scalar(3)
         gather(0, 0, S)
-        for a in range(last):
-            round_pair(2 * a + 1)
-            for lo, hi in HALVES:
-                gather(2 * a + 1, lo, hi)
-            round_pair(2 * a + 2)
-            for lo, hi in HALVES:
-                interleave(nc.vector.tensor_copy, a, lo, hi)
-            for lo, hi in HALVES:
-                quantize(a, lo, hi)
-            gather(2 * a + 2, 0, S)
-
-        round_pair(PAIRS - 1)
+        round_vector(1)
+        gather(1, 0, S // 2)
+        gather(1, S // 2, S)
+        interleave(nc.vector.tensor_copy, 0, 0, S // 2)
+        interleave(nc.vector.tensor_copy, 0, S // 2, S)
+        round_vector(2)
+        round_scalar(4)
+        quantize(0, 0, S // 2)
+        quantize(0, S // 2, S)
+        gather(2, 0, S)
+        round_scalar(5)
+        gather(3, 0, S // 2)
+        gather(3, S // 2, S)
+        interleave(nc.vector.tensor_copy, 1, 0, S // 2)
+        interleave(nc.vector.tensor_copy, 1, S // 2, S)
+        quantize(1, 0, S // 2)
+        gather(4, 0, S)
+        round_vector(5)
+        quantize(1, S // 2, S)
         for s in range(len(SLICES)):
             for a in range(last):
                 multiply(a, s)

@@ -20,18 +20,16 @@ K_PASS = P * PACK
 PASSES = K // K_PASS
 PAIRS = 2 * PASSES
 SLICES = ((0, 128), (128, 256), (256, 384), (384, 512))
-VECTOR_SHARE = (704, 672, 64, 0, 0, 96)
+VECTOR_SHARE = (704, 672, 64, 0, 0, 288)
 
 
-GPSIMD_SHARE = {(3, 0): 384, (4, 0): 128, (4, 512): 96, (5, 512): 160}
+GPSIMD_SHARE = {(3, 0): 384, (4, 0): 128, (4, 512): 96}
 
 
 def load_chunks(pair):
     if pair < 4:
         return ((0, T),)
-    if pair == 4:
-        return ((0, T // 2), (T // 2, T))
-    return ((0, T // 2), (T // 2, 3 * T // 4), (3 * T // 4, T))
+    return ((0, T // 2), (T // 2, T))
 
 
 def tile_picked_pool_lin_silu_sub_e_kernel(tc, xT, w_words, w_scales, b, offs, out):

from contextlib import ExitStack

import concourse.mybir as mybir

K, T, D, S, V, N = 1536, 1024, 8, 512, 64, 128
FLOPS = 2 * K * N * S

F32 = mybir.dt.float32
BF16 = mybir.dt.bfloat16
I32 = mybir.dt.int32
U32 = mybir.dt.uint32
U16 = mybir.dt.uint16
U8 = mybir.dt.uint8
FP8X4 = mybir.dt.float8_e4m3fn_x4
SILU = mybir.ActivationFunctionType.Silu

P = 128
PACK = 4
K_PASS = P * PACK
PASSES = K // K_PASS
PAIRS = 2 * PASSES
SLICES = ((0, 128), (128, 256), (256, 384), (384, 512))
VECTOR_SHARE = (704, 672, 64, 0, 0, 288)


GPSIMD_SHARE = {(3, 0): 384, (4, 0): 128, (4, 512): 96}


def load_chunks(pair):
    if pair < 4:
        return ((0, T),)
    return ((0, T // 2), (T // 2, T))


def tile_picked_pool_lin_silu_sub_e_kernel(tc, xT, w_words, w_scales, b, offs, out):
    nc = tc.nc
    with ExitStack() as ctx:
        keep = ctx.enter_context(tc.tile_pool(name="keep", bufs=1))
        psum = ctx.enter_context(tc.psum_pool(name="psum", bufs=1))

        offsets = keep.tile([P, S // 16], U16, name="offsets")
        w_codes = keep.tile([P, PASSES, N], U32, name="w_codes", align_bytes=64)
        w_plane = keep.tile([P, PASSES, N], U8, name="w_plane", align_bytes=64)
        bias = keep.tile([P, 1], F32, name="bias")
        warm = keep.tile([P, 2], F32, name="warm")
        pooled = keep.tile([P, V], F32, name="pooled")
        raw = [keep.tile([P, 2, T], F32, name=f"raw{i}") for i in range(PAIRS)]
        words = [keep.tile([P, T, 2], BF16, name=f"words{i}", align_bytes=64) for i in range(PAIRS)]
        halves = [keep.tile([P, 2, S], U32, name=f"halves{a}", align_bytes=64) for a in range(PASSES)]
        picked = [keep.tile([P, S, PACK], BF16, name=f"picked{a}", align_bytes=64) for a in range(PASSES)]
        x_codes = [keep.tile([P, S], U32, name=f"x_codes{a}", align_bytes=64) for a in range(PASSES)]
        x_plane = [keep.tile([P, S], U8, name=f"x_plane{a}", align_bytes=64) for a in range(PASSES)]
        acc = [psum.tile([P, hi - lo], F32, name=f"acc{lo}") for lo, hi in SLICES]
        act = [keep.tile([P, hi - lo], F32, name=f"act{lo}") for lo, hi in SLICES]

        nc.vector.memset(warm[:, 0:1], 0.0)
        nc.vector.memset(w_plane[:].rearrange("p a n -> p (a n)").bitcast(I32), 0)
        nc.scalar.activation(warm[:, 1:2], warm[:, 0:1], SILU)

        x_rows = xT.rearrange("(a p u e) t -> a u p e t", a=PASSES, p=P, u=2)

        def load(i):
            for lo, hi in load_chunks(i):
                nc.sync.dma_start(out=raw[i][:, :, lo:hi], in_=x_rows[i // 2, i % 2][:, :, lo:hi])

        load(0)
        nc.sync.dma_start(offsets[:], offs)
        for i in range(1, PAIRS):
            load(i)
        nc.sync.dma_start(
            out=w_codes[:].bitcast(I32),
            in_=w_words.rearrange("a p n r -> p a (n r)").bitcast(I32),
        )
        scale_rows = w_scales.bitcast(I32).rearrange("a (q r) n -> r q a n", r=4)
        for r in range(4):
            nc.sync.dma_start(out=w_plane[r:P:32].bitcast(I32), in_=scale_rows[r])
        nc.sync.dma_start(out=bias[:], in_=b)

        def round_scalar(i):
            cut = T - VECTOR_SHARE[i]
            for lo, hi in load_chunks(i):
                hi = min(hi, cut)
                mid = hi - GPSIMD_SHARE.get((i, lo), 0)
                nc.scalar.copy(words[i][:, lo:mid, :], raw[i][:, :, lo:mid].rearrange("p e t -> p t e"))
                if mid < hi:
                    nc.gpsimd.tensor_scalar(
                        words[i][:, mid:hi, :],
                        raw[i][:, :, mid:hi].rearrange("p e t -> p t e"),
                        1.0,
                        0.0,
                        mybir.AluOpType.mult,
                        mybir.AluOpType.add,
                    )

        def round_vector(i):
            cut = T - VECTOR_SHARE[i]
            nc.vector.tensor_copy(words[i][:, cut:, :], raw[i][:, :, cut:].rearrange("p e t -> p t e"))

        def gather(i, lo, hi):
            window = words[i][:].rearrange("p t e -> p (t e)").bitcast(U32)
            nc.vector.tensor_copy(halves[i // 2][:, i % 2, lo:hi], window.indirect(offsets[:, lo // 16 : hi // 16]))

        def interleave(copy, a, lo, hi):
            src = halves[a][:].bitcast(F32).rearrange("p u s -> p s u")
            dst = picked[a][:].bitcast(F32)
            copy(dst[:, lo:hi], src[:, lo:hi])

        def quantize(a, lo, hi):
            nc.vector.quantize_mx(
                out=x_codes[a][:, lo:hi].bitcast(FP8X4),
                scales=x_plane[a][:, lo:hi],
                in_=picked[a][:, lo:hi, :].rearrange("p s j -> p (s j)"),
            )

        def multiply(a, s):
            lo, hi = SLICES[s]
            nc.tensor.matmul_mx(
                out=acc[s][:],
                lhsT=w_codes[:, a, :].bitcast(FP8X4),
                lhsT_scale=w_plane[:, a, :],
                rhs=x_codes[a][:, lo:hi].bitcast(FP8X4),
                rhs_scale=x_plane[a][:, lo:hi],
                start=(a == 0),
                stop=(a == PASSES - 1),
            )

        last = PASSES - 1
        round_scalar(0)
        round_vector(0)
        round_scalar(1)
        round_scalar(2)
        round_scalar(3)
        gather(0, 0, S)
        round_vector(1)
        gather(1, 0, S // 2)
        gather(1, S // 2, S)
        interleave(nc.vector.tensor_copy, 0, 0, S // 2)
        interleave(nc.vector.tensor_copy, 0, S // 2, S)
        round_vector(2)
        round_scalar(4)
        quantize(0, 0, S // 2)
        quantize(0, S // 2, S)
        gather(2, 0, S)
        round_scalar(5)
        gather(3, 0, S // 2)
        gather(3, S // 2, S)
        interleave(nc.vector.tensor_copy, 1, 0, S // 2)
        interleave(nc.vector.tensor_copy, 1, S // 2, S)
        quantize(1, 0, S // 2)
        gather(4, 0, S)
        round_vector(5)
        quantize(1, S // 2, S)
        for s in range(len(SLICES)):
            for a in range(last):
                multiply(a, s)
        for lo, hi in SLICES:
            gather(PAIRS - 1, lo, hi)
            interleave(nc.scalar.copy, last, lo, hi)
        for s in range(len(SLICES)):
            quantize(last, *SLICES[s])
            multiply(last, s)
            nc.scalar.activation(act[s][:], acc[s][:], SILU, bias=bias[:])
        for s, (lo, hi) in enumerate(SLICES):
            nc.vector.tensor_reduce(
                out=pooled[:, lo // D : hi // D],
                in_=act[s][:].rearrange("p (v d) -> p v d", d=D),
                axis=mybir.AxisListType.X,
                op=mybir.AluOpType.max,
            )
        nc.sync.dma_start(out=out, in_=pooled[:])
